import numpy as np
CORES = [43,35,59,51,47,39,63,55]
N = 8
GR, GC, W, CW, TIMES = 2, 4, 256, 4, 2
def setup_inputs(rng):
    return {"x": rng.standard_normal((N, 128, W), dtype=np.float32)}
def reference(x):
    X = x.astype(np.float64).reshape(GR, GC, 128, W)
    g = np.concatenate([np.concatenate(list(X[i]), axis=1) for i in range(GR)], axis=0)
    for _ in range(TIMES):
        g = CW * g + np.roll(g, 1, 0) + np.roll(g, -1, 0) + np.roll(g, 1, 1) + np.roll(g, -1, 1)
    return {"y": np.stack([g[128 * (r // GC):128 * (r // GC) + 128, W * (r % GC):W * (r % GC) + W] for r in range(N)]).astype(np.float32 if x.dtype != np.float64 else np.float64)}

@@ -1,0 +1,136 @@
+from concourse.bass import DstId, RemoteDMATransfer
+from concourse.mybir import AluOpType
+
+F = "float32"
+SCRATCH = {
+    "XE": ("sbuf", [128, 264], F),
+    "Z1": ("sbuf", [128, 256], F),
+    "Z2": ("sbuf", [128, 256], F),
+    "Y": ("sbuf", [128, 256], F),
+    "PA0": ("sbuf", [128, 133], F),
+    "PA1": ("sbuf", [128, 131], F),
+    "D0": ("dram", [128 * 133], F),
+    "D1": ("dram", [128 * 131], F),
+    "M0": ("sbuf", [128, 132], F),
+    "M1": ("sbuf", [128, 130], F),
+    "CC": ("sbuf", [128, 128], F),
+    "LQ": ("sbuf", [128, 128], F),
+    "Q": ("sbuf", [128, 256], F),
+    "QL": ("sbuf", [128, 256], F),
+    "HB": ("sbuf", [128, 4], F),
+    "DB": ("sbuf", [128, 4], F),
+    "P": ("psum", [128, 256], F),
+}
+SEMAPHORES = ["ldx", "ldq", "ldm0", "ldm1", "std0", "std1", "vp0", "vp1", "vq", "vx", "vz1", "vz2", "vc", "ve", "vy",
+              "arrh", "arrq", "sent", "pe", "st"]
+
+W_FILLS = [
+    [("LQ", 96, 128, 0, 128, 0), ("CC", 0, 128, 0, 128, 0)],
+    [("LQ", 96, 128, 0, 1, 2), ("LQ", 96, 126, 1, 2, 1), ("LQ", 96, 124, 127, 128, 2), ("LQ", 96, 121, 126, 127, 1),
+     ("CC", 0, 1, 127, 128, 2), ("CC", 96, 128, 0, 1, 2)],
+    [("LQ", 96, 126, 0, 1, 8), ("LQ", 96, 125, 1, 2, 0), ("LQ", 96, 122, 127, 128, 1), ("LQ", 96, 120, 126, 127, 0),
+     ("CC", 96, 127, 0, 1, 0)],
+    [("LQ", 96, 125, 0, 1, 1), ("LQ", 96, 121, 127, 128, 8)],
+    [("LQ", 96, 124, 0, 1, 0), ("LQ", 96, 120, 127, 128, 0)],
+]
+
+
+def _fills(g, T, levels, sem):
+    n = 0
+    for i, level in enumerate(levels):
+        if i:
+            g.vector.wait_ge(sem, n)
+        for (b, p0, p1, c0, c1, v) in level:
+            g.vector.memset(T[b][p0:p1, c0:c1], float(v)).then_inc(sem, 1)
+            n += 1
+    return n
+
+
+def rank_program(g, core, T, topo):
+    rank = T.rank_of(core)
+    if rank is None:
+        return
+    S = T.sem
+    add = AluOpType.add
+
+    def nb(dr, dc):
+        return T.cores[((rank // 4 + dr) % 2) * 4 + (rank % 4 + dc) % 4]
+
+    def did(c):
+        rid, pid, _ = topo.addr(c)
+        return DstId(rid=rid, pnc=pid)
+
+    x = T.x
+    for (c0, c1, st, v) in ((5, 133, 1, 0), (0, 5, 4, 1), (1, 4, 2, 8), (2, 3, 1, 20)):
+        g.vector.memset(T.PA0[:, c0:c1:st], float(v)).then_inc(S.vp0, 1)
+    g.vector.memset(T.Q[96:128, 0:4], 0.0).then_inc(S.vq, 1)
+    g.vector.memset(T.Q[96:128, 252:256], 0.0).then_inc(S.vq, 1)
+    for (c0, c1, st, v) in ((3, 131, 1, 0), (0, 3, 2, 2), (1, 2, 1, 8)):
+        g.vector.memset(T.PA1[:, c0:c1:st], float(v)).then_inc(S.vp1, 1)
+    g.vector.memset(T.XE[:, 0:4], 0.0).then_inc(S.vx, 1)
+    g.vector.memset(T.XE[:, 260:264], 0.0).then_inc(S.vx, 1)
+
+    g.sync.dma_start(T.XE[:, 4:260], x[:, :]).then_inc(S.ldx, 16)
+    g.sync.wait_ge(S.vp0, 4)
+    g.sync.dma_start(T.D0[0:128 * 133], T.PA0[:, :]).then_inc(S.std0, 16)
+    g.sync.wait_ge(S.vq, 2)
+    g.sync.dma_start(T.Q[120:122, :], x[0:2, :]).then_inc(S.ldq, 16)
+    g.sync.dma_start(T.Q[127:128, 0:255], x[127:128, 1:256]).then_inc(S.ldq, 16)
+    g.sync.dma_start(T.Q[123:124, 0:255], x[0:1, 1:256]).then_inc(S.ldq, 16)
+    g.sync.wait_ge(S.std0, 16)
+    g.sync.dma_start(T.M0[:, :], T.D0[0:128 * 132]).then_inc(S.ldm0, 16)
+
+    g.scalar.wait_ge(S.vq, 2)
+    g.scalar.dma_start(T.Q[0:120, :], x[0:120, :]).then_inc(S.ldq, 16)
+    g.scalar.wait_ge(S.vp1, 3)
+    g.scalar.dma_start(T.D1[0:128 * 131], T.PA1[:, :]).then_inc(S.std1, 16)
+    g.scalar.dma_start(T.Q[124:126, :], x[126:128, :]).then_inc(S.ldq, 16)
+    g.scalar.dma_start(T.Q[126:127, 1:256], x[127:128, 0:255]).then_inc(S.ldq, 16)
+    g.scalar.dma_start(T.Q[122:123, 1:256], x[0:1, 0:255]).then_inc(S.ldq, 16)
+    g.scalar.wait_ge(S.std1, 16)
+    g.scalar.dma_start(T.M1[:, :], T.D1[0:128 * 130]).then_inc(S.ldm1, 16)
+
+    g.vector.wait_ge(S.vx, 2)
+    g.vector.wait_ge(S.ldx, 16)
+    g.vector.tensor_tensor(out=T.Z1[:, :], in0=T.XE[:, 3:259], in1=T.XE[:, 5:261], op=add).then_inc(S.vz1, 1)
+    g.vector.tensor_tensor(out=T.Z2[:, :], in0=T.XE[:, 2:258], in1=T.XE[:, 6:262], op=add).then_inc(S.vz2, 1)
+    nw = _fills(g, T, W_FILLS, S.vc)
+
+    g.wait_ge(S.ldx, 16)
+    g.remote_dma_fused([
+        RemoteDMATransfer(dst_ids=[did(nb(0, -1)), did(nb(1, -1))], dma_engine_mask=0x0F, remote_sem=S.arrh,
+                          srcs=[T.XE[:, 4:6]], dsts=[T.HB[:, 2:4], T.DB[:, 2:4]], alu_op=0),
+        RemoteDMATransfer(dst_ids=[did(nb(0, 1)), did(nb(1, 1))], dma_engine_mask=0xF0, remote_sem=S.arrh,
+                          srcs=[T.XE[:, 258:260]], dsts=[T.HB[:, 0:2], T.DB[:, 0:2]], alu_op=0),
+    ], local_sem=S.sent)
+    g.wait_ge(S.vq, 2)
+    g.wait_ge(S.ldq, 112)
+    rid, pid, _ = topo.addr(nb(1, 0))
+    g.remote_dma(T.QL[:, :], T.Q[:, :], S.arrq, S.sent, pid, rid, 0xFFFF)
+
+    pe = g.tensor
+    pe.wait_ge(S.ldx, 16)
+    pe.wait_ge(S.ldm0, 16)
+    pe.matmul(out=T.P[:, :], lhsT=T.M0[:, 2:130], rhs=T.XE[:, 4:260], start=True, stop=False)
+    pe.wait_ge(S.ldm1, 16)
+    pe.wait_ge(S.vz1, 1)
+    pe.matmul(out=T.P[:, :], lhsT=T.M1[:, 1:129], rhs=T.Z1[:, :], start=False, stop=False)
+    pe.wait_ge(S.vc, nw)
+    pe.wait_ge(S.arrq, 16)
+    pe.matmul(out=T.P[:, :], lhsT=T.LQ[96:128, :], rhs=T.QL[96:128, :], start=False, stop=False)
+    pe.wait_ge(S.arrh, 16)
+    pe.matmul(out=T.P[:, 0:256:255], lhsT=T.M1[:, 1:129], rhs=T.HB[:, 1:3], start=False, stop=False)
+    pe.matmul(out=T.P[:, 0:256:255], lhsT=T.CC[:, :], rhs=T.DB[:, 1:3], start=False, stop=True).then_inc(S.pe, 1)
+
+    g.vector.wait_ge(S.vz2, 1)
+    g.vector.wait_ge(S.arrh, 16)
+    g.vector.tensor_tensor(out=T.Z2[:, 0:2], in0=T.Z2[:, 0:2], in1=T.HB[:, 0:2], op=add).then_inc(S.ve, 1)
+    g.vector.tensor_tensor(out=T.Z2[:, 254:256], in0=T.Z2[:, 254:256], in1=T.HB[:, 2:4], op=add).then_inc(S.ve, 1)
+    g.vector.wait_ge(S.ve, 2)
+    g.vector.wait_ge(S.pe, 1)
+    g.vector.tensor_tensor(out=T.Y[:, :], in0=T.P[:, :], in1=T.Z2[:, :], op=add).then_inc(S.vy, 1)
+
+    g.sync.wait_ge(S.vy, 1)
+    g.sync.dma_start(T.y[:, :], T.Y[:, :]).then_inc(S.st, 16)
+    g.sync.wait_ge(S.st, 16)
+    g.wait_ge(S.sent, 24)

@@ -7,10 +7,8 @@ SCRATCH = {
     "Z1": ("sbuf", [128, 256], F),
     "Z2": ("sbuf", [128, 256], F),
     "Y": ("sbuf", [128, 256], F),
-    "PA0": ("sbuf", [128, 133], F),
-    "PA1": ("sbuf", [128, 131], F),
-    "D0": ("dram", [128 * 133], F),
-    "D1": ("dram", [128 * 131], F),
+    "D0": ("dram", [64 * 69], F),
+    "D1": ("dram", [64 * 67], F),
     "M0": ("sbuf", [128, 132], F),
     "M1": ("sbuf", [128, 130], F),
     "CC": ("sbuf", [128, 128], F),
@@ -21,8 +19,8 @@ SCRATCH = {
     "DB": ("sbuf", [128, 4], F),
     "P": ("psum", [128, 256], F),
 }
-SEMAPHORES = ["ldx", "ldq", "ldm0", "ldm1", "std0", "std1", "vp0", "vp1", "vq", "vx", "vz1", "vz2", "vc", "ve", "vy",
-              "arrh", "arrq", "sent", "pe", "st"]
+SEMAPHORES = ["ldx", "ldq", "ldm0", "ldm1", "std0", "std1", "vp0", "vp1", "vq", "vx", "vz1", "vm", "vr",
+              "vz2", "vc", "ve", "vy", "arrh", "arrq", "sent", "pe", "st"]
 
 W_FILLS = [
     [("LQ", 96, 128, 0, 128, 0), ("CC", 0, 128, 0, 128, 0)],
@@ -61,34 +59,41 @@ def rank_program(g, core, T, topo):
         return DstId(rid=rid, pnc=pid)
 
     x = T.x
-    for (c0, c1, st, v) in ((5, 133, 1, 0), (0, 5, 4, 1), (1, 4, 2, 8), (2, 3, 1, 20)):
-        g.vector.memset(T.PA0[:, c0:c1:st], float(v)).then_inc(S.vp0, 1)
+    for (c0, c1, st, v) in ((5, 69, 1, 0), (0, 5, 4, 1), (1, 4, 2, 8), (2, 3, 1, 20)):
+        g.vector.memset(T.Q[0:96, c0:c1:st], float(v)).then_inc(S.vp0, 1)
     g.vector.memset(T.Q[96:128, 0:4], 0.0).then_inc(S.vq, 1)
     g.vector.memset(T.Q[96:128, 252:256], 0.0).then_inc(S.vq, 1)
-    for (c0, c1, st, v) in ((3, 131, 1, 0), (0, 3, 2, 2), (1, 2, 1, 8)):
-        g.vector.memset(T.PA1[:, c0:c1:st], float(v)).then_inc(S.vp1, 1)
+    for (c0, c1, st, v) in ((72, 136, 1, 0), (69, 72, 2, 2), (70, 71, 1, 8)):
+        g.vector.memset(T.Q[0:96, c0:c1:st], float(v)).then_inc(S.vp1, 1)
+    g.vector.memset(T.Q[0:96, 136:256], 0.0).then_inc(S.vr, 1)
+    g.vector.memset(T.M0[:, :], 0.0).then_inc(S.vm, 1)
+    g.vector.memset(T.M1[:, :], 0.0).then_inc(S.vm, 1)
     g.vector.memset(T.XE[:, 0:4], 0.0).then_inc(S.vx, 1)
     g.vector.memset(T.XE[:, 260:264], 0.0).then_inc(S.vx, 1)
 
     g.sync.dma_start(T.XE[:, 4:260], x[:, :]).then_inc(S.ldx, 16)
     g.sync.wait_ge(S.vp0, 4)
-    g.sync.dma_start(T.D0[0:128 * 133], T.PA0[:, :]).then_inc(S.std0, 16)
+    g.sync.dma_start(T.D0[0:64 * 69], T.Q[0:64, 0:69]).then_inc(S.std0, 16)
     g.sync.wait_ge(S.vq, 2)
     g.sync.dma_start(T.Q[120:122, :], x[0:2, :]).then_inc(S.ldq, 16)
     g.sync.dma_start(T.Q[127:128, 0:255], x[127:128, 1:256]).then_inc(S.ldq, 16)
     g.sync.dma_start(T.Q[123:124, 0:255], x[0:1, 1:256]).then_inc(S.ldq, 16)
+    g.sync.wait_ge(S.vm, 2)
     g.sync.wait_ge(S.std0, 16)
-    g.sync.dma_start(T.M0[:, :], T.D0[0:128 * 132]).then_inc(S.ldm0, 16)
+    g.sync.dma_start(T.M0[0:64, 0:68], T.D0[0:64 * 68]).then_inc(S.ldm0, 16)
+    g.sync.dma_start(T.M0[64:128, 64:132], T.D0[0:64 * 68]).then_inc(S.ldm0, 16)
 
     g.scalar.wait_ge(S.vq, 2)
-    g.scalar.dma_start(T.Q[0:120, :], x[0:120, :]).then_inc(S.ldq, 16)
-    g.scalar.wait_ge(S.vp1, 3)
-    g.scalar.dma_start(T.D1[0:128 * 131], T.PA1[:, :]).then_inc(S.std1, 16)
+    g.scalar.dma_start(T.Q[96:120, :], x[96:120, :]).then_inc(S.ldq, 16)
     g.scalar.dma_start(T.Q[124:126, :], x[126:128, :]).then_inc(S.ldq, 16)
     g.scalar.dma_start(T.Q[126:127, 1:256], x[127:128, 0:255]).then_inc(S.ldq, 16)
     g.scalar.dma_start(T.Q[122:123, 1:256], x[0:1, 0:255]).then_inc(S.ldq, 16)
+    g.scalar.wait_ge(S.vp1, 3)
+    g.scalar.dma_start(T.D1[0:64 * 67], T.Q[0:64, 69:136]).then_inc(S.std1, 16)
+    g.scalar.wait_ge(S.vm, 2)
     g.scalar.wait_ge(S.std1, 16)
-    g.scalar.dma_start(T.M1[:, :], T.D1[0:128 * 130]).then_inc(S.ldm1, 16)
+    g.scalar.dma_start(T.M1[0:64, 0:66], T.D1[0:64 * 66]).then_inc(S.ldm1, 16)
+    g.scalar.dma_start(T.M1[64:128, 64:130], T.D1[0:64 * 66]).then_inc(S.ldm1, 16)
 
     g.vector.wait_ge(S.vx, 2)
     g.vector.wait_ge(S.ldx, 16)
@@ -103,6 +108,9 @@ def rank_program(g, core, T, topo):
         RemoteDMATransfer(dst_ids=[did(nb(0, 1)), did(nb(1, 1))], dma_engine_mask=0xF0, remote_sem=S.arrh,
                           srcs=[T.XE[:, 258:260]], dsts=[T.HB[:, 0:2], T.DB[:, 0:2]], alu_op=0),
     ], local_sem=S.sent)
+    g.wait_ge(S.vp0, 4)
+    g.wait_ge(S.vp1, 3)
+    g.wait_ge(S.vr, 1)
     g.wait_ge(S.vq, 2)
     g.wait_ge(S.ldq, 112)
     rid, pid, _ = topo.addr(nb(1, 0))
@@ -110,9 +118,9 @@ def rank_program(g, core, T, topo):
 
     pe = g.tensor
     pe.wait_ge(S.ldx, 16)
-    pe.wait_ge(S.ldm0, 16)
+    pe.wait_ge(S.ldm0, 32)
     pe.matmul(out=T.P[:, :], lhsT=T.M0[:, 2:130], rhs=T.XE[:, 4:260], start=True, stop=False)
-    pe.wait_ge(S.ldm1, 16)
+    pe.wait_ge(S.ldm1, 32)
     pe.wait_ge(S.vz1, 1)
     pe.matmul(out=T.P[:, :], lhsT=T.M1[:, 1:129], rhs=T.Z1[:, :], start=False, stop=False)
     pe.wait_ge(S.vc, nw)

@@ -33,10 +33,9 @@ W_FILLS = [
 ]
 
 
-def _fills(g, T, levels, sem):
-    n = 0
-    for i, level in enumerate(levels):
-        if i:
+def _fills(g, T, levels, sem, n):
+    for level in levels:
+        if n:
             g.vector.wait_ge(sem, n)
         for (b, p0, p1, c0, c1, v) in level:
             g.vector.memset(T[b][p0:p1, c0:c1], float(v)).then_inc(sem, 1)
@@ -59,47 +58,50 @@ def rank_program(g, core, T, topo):
         return DstId(rid=rid, pnc=pid)
 
     x = T.x
-    for (c0, c1, st, v) in ((5, 69, 1, 0), (0, 5, 4, 1), (1, 4, 2, 8), (2, 3, 1, 20)):
-        g.vector.memset(T.Q[0:96, c0:c1:st], float(v)).then_inc(S.vp0, 1)
-    g.vector.memset(T.Q[96:128, 0:4], 0.0).then_inc(S.vq, 1)
-    g.vector.memset(T.Q[96:128, 252:256], 0.0).then_inc(S.vq, 1)
     for (c0, c1, st, v) in ((72, 136, 1, 0), (69, 72, 2, 2), (70, 71, 1, 8)):
         g.vector.memset(T.Q[0:96, c0:c1:st], float(v)).then_inc(S.vp1, 1)
-    g.vector.memset(T.Q[0:96, 136:256], 0.0).then_inc(S.vr, 1)
-    g.vector.memset(T.M0[:, :], 0.0).then_inc(S.vm, 1)
+    g.vector.memset(T.Q[96:128, 0:4], 0.0).then_inc(S.vq, 1)
+    g.vector.memset(T.Q[96:128, 252:256], 0.0).then_inc(S.vq, 1)
+    for (c0, c1, st, v) in ((5, 69, 1, 0), (0, 5, 4, 1), (1, 4, 2, 8), (2, 3, 1, 20)):
+        g.vector.memset(T.Q[0:96, c0:c1:st], float(v)).then_inc(S.vp0, 1)
     g.vector.memset(T.M1[:, :], 0.0).then_inc(S.vm, 1)
+    g.vector.memset(T.M0[:, :], 0.0).then_inc(S.vm, 1)
+    g.vector.memset(T.Q[0:96, 136:256], 0.0).then_inc(S.vr, 1)
     g.vector.memset(T.XE[:, 0:4], 0.0).then_inc(S.vx, 1)
     g.vector.memset(T.XE[:, 260:264], 0.0).then_inc(S.vx, 1)
+    nw = _fills(g, T, W_FILLS[:1], S.vc, 0)
 
     g.sync.dma_start(T.XE[:, 4:260], x[:, :]).then_inc(S.ldx, 16)
-    g.sync.wait_ge(S.vp0, 4)
-    g.sync.dma_start(T.D0[0:64 * 69], T.Q[0:64, 0:69]).then_inc(S.std0, 16)
+    g.sync.wait_ge(S.vp1, 3)
+    g.sync.dma_start(T.D1[0:64 * 67], T.Q[0:64, 69:136]).then_inc(S.std1, 16)
     g.sync.wait_ge(S.vq, 2)
     g.sync.dma_start(T.Q[120:122, :], x[0:2, :]).then_inc(S.ldq, 16)
     g.sync.dma_start(T.Q[127:128, 0:255], x[127:128, 1:256]).then_inc(S.ldq, 16)
     g.sync.dma_start(T.Q[123:124, 0:255], x[0:1, 1:256]).then_inc(S.ldq, 16)
     g.sync.wait_ge(S.vm, 2)
+    g.sync.wait_ge(S.std1, 16)
+    g.sync.dma_start(T.M1[0:64, 0:66], T.D1[0:64 * 66]).then_inc(S.ldm1, 16)
     g.sync.wait_ge(S.std0, 16)
     g.sync.dma_start(T.M0[0:64, 0:68], T.D0[0:64 * 68]).then_inc(S.ldm0, 16)
-    g.sync.dma_start(T.M0[64:128, 64:132], T.D0[0:64 * 68]).then_inc(S.ldm0, 16)
 
     g.scalar.wait_ge(S.vq, 2)
     g.scalar.dma_start(T.Q[96:120, :], x[96:120, :]).then_inc(S.ldq, 16)
     g.scalar.dma_start(T.Q[124:126, :], x[126:128, :]).then_inc(S.ldq, 16)
     g.scalar.dma_start(T.Q[126:127, 1:256], x[127:128, 0:255]).then_inc(S.ldq, 16)
     g.scalar.dma_start(T.Q[122:123, 1:256], x[0:1, 0:255]).then_inc(S.ldq, 16)
-    g.scalar.wait_ge(S.vp1, 3)
-    g.scalar.dma_start(T.D1[0:64 * 67], T.Q[0:64, 69:136]).then_inc(S.std1, 16)
+    g.scalar.wait_ge(S.vp0, 4)
+    g.scalar.dma_start(T.D0[0:64 * 69], T.Q[0:64, 0:69]).then_inc(S.std0, 16)
     g.scalar.wait_ge(S.vm, 2)
     g.scalar.wait_ge(S.std1, 16)
-    g.scalar.dma_start(T.M1[0:64, 0:66], T.D1[0:64 * 66]).then_inc(S.ldm1, 16)
     g.scalar.dma_start(T.M1[64:128, 64:130], T.D1[0:64 * 66]).then_inc(S.ldm1, 16)
+    g.scalar.wait_ge(S.std0, 16)
+    g.scalar.dma_start(T.M0[64:128, 64:132], T.D0[0:64 * 68]).then_inc(S.ldm0, 16)
 
     g.vector.wait_ge(S.vx, 2)
     g.vector.wait_ge(S.ldx, 16)
     g.vector.tensor_tensor(out=T.Z1[:, :], in0=T.XE[:, 3:259], in1=T.XE[:, 5:261], op=add).then_inc(S.vz1, 1)
+    nw = _fills(g, T, W_FILLS[1:], S.vc, nw)
     g.vector.tensor_tensor(out=T.Z2[:, :], in0=T.XE[:, 2:258], in1=T.XE[:, 6:262], op=add).then_inc(S.vz2, 1)
-    nw = _fills(g, T, W_FILLS, S.vc)
 
     g.wait_ge(S.ldx, 16)
     g.remote_dma_fused([
@@ -117,12 +119,12 @@ def rank_program(g, core, T, topo):
     g.remote_dma(T.QL[:, :], T.Q[:, :], S.arrq, S.sent, pid, rid, 0xFFFF)
 
     pe = g.tensor
-    pe.wait_ge(S.ldx, 16)
-    pe.wait_ge(S.ldm0, 32)
-    pe.matmul(out=T.P[:, :], lhsT=T.M0[:, 2:130], rhs=T.XE[:, 4:260], start=True, stop=False)
     pe.wait_ge(S.ldm1, 32)
     pe.wait_ge(S.vz1, 1)
-    pe.matmul(out=T.P[:, :], lhsT=T.M1[:, 1:129], rhs=T.Z1[:, :], start=False, stop=False)
+    pe.matmul(out=T.P[:, :], lhsT=T.M1[:, 1:129], rhs=T.Z1[:, :], start=True, stop=False)
+    pe.wait_ge(S.ldx, 16)
+    pe.wait_ge(S.ldm0, 32)
+    pe.matmul(out=T.P[:, :], lhsT=T.M0[:, 2:130], rhs=T.XE[:, 4:260], start=False, stop=False)
     pe.wait_ge(S.vc, nw)
     pe.wait_ge(S.arrq, 16)
     pe.matmul(out=T.P[:, :], lhsT=T.LQ[96:128, :], rhs=T.QL[96:128, :], start=False, stop=False)

from concourse.bass import DstId, RemoteDMATransfer
from concourse.mybir import AluOpType

F = "float32"
SCRATCH = {
    "XE": ("sbuf", [128, 264], F),
    "Z1": ("sbuf", [128, 256], F),
    "Z2": ("sbuf", [128, 256], F),
    "Y": ("sbuf", [128, 256], F),
    "D0": ("dram", [64 * 69], F),
    "D1": ("dram", [64 * 67], F),
    "M0": ("sbuf", [128, 132], F),
    "M1": ("sbuf", [128, 130], F),
    "CC": ("sbuf", [128, 128], F),
    "LQ": ("sbuf", [128, 128], F),
    "Q": ("sbuf", [128, 256], F),
    "QL": ("sbuf", [128, 256], F),
    "HB": ("sbuf", [128, 4], F),
    "DB": ("sbuf", [128, 4], F),
    "P": ("psum", [128, 256], F),
}
SEMAPHORES = ["ldx", "ldq", "ldm0", "ldm1", "std0", "std1", "vp0", "vp1", "vq", "vx", "vz1", "vm", "vr",
              "vz2", "vc", "ve", "vy", "arrh", "arrq", "sent", "pe", "st"]

W_FILLS = [
    [("LQ", 96, 128, 0, 128, 0), ("CC", 0, 128, 0, 128, 0)],
    [("LQ", 96, 128, 0, 1, 2), ("LQ", 96, 126, 1, 2, 1), ("LQ", 96, 124, 127, 128, 2), ("LQ", 96, 121, 126, 127, 1),
     ("CC", 0, 1, 127, 128, 2), ("CC", 96, 128, 0, 1, 2)],
    [("LQ", 96, 126, 0, 1, 8), ("LQ", 96, 125, 1, 2, 0), ("LQ", 96, 122, 127, 128, 1), ("LQ", 96, 120, 126, 127, 0),
     ("CC", 96, 127, 0, 1, 0)],
    [("LQ", 96, 125, 0, 1, 1), ("LQ", 96, 121, 127, 128, 8)],
    [("LQ", 96, 124, 0, 1, 0), ("LQ", 96, 120, 127, 128, 0)],
]


def _fills(g, T, levels, sem, n):
    for level in levels:
        if n:
            g.vector.wait_ge(sem, n)
        for (b, p0, p1, c0, c1, v) in level:
            g.vector.memset(T[b][p0:p1, c0:c1], float(v)).then_inc(sem, 1)
            n += 1
    return n


def rank_program(g, core, T, topo):
    rank = T.rank_of(core)
    if rank is None:
        return
    S = T.sem
    add = AluOpType.add

    def nb(dr, dc):
        return T.cores[((rank // 4 + dr) % 2) * 4 + (rank % 4 + dc) % 4]

    def did(c):
        rid, pid, _ = topo.addr(c)
        return DstId(rid=rid, pnc=pid)

    x = T.x
    for (c0, c1, st, v) in ((72, 136, 1, 0), (69, 72, 2, 2), (70, 71, 1, 8)):
        g.vector.memset(T.Q[0:96, c0:c1:st], float(v)).then_inc(S.vp1, 1)
    g.vector.memset(T.Q[96:128, 0:4], 0.0).then_inc(S.vq, 1)
    g.vector.memset(T.Q[96:128, 252:256], 0.0).then_inc(S.vq, 1)
    for (c0, c1, st, v) in ((5, 69, 1, 0), (0, 5, 4, 1), (1, 4, 2, 8), (2, 3, 1, 20)):
        g.vector.memset(T.Q[0:96, c0:c1:st], float(v)).then_inc(S.vp0, 1)
    g.vector.memset(T.M1[:, :], 0.0).then_inc(S.vm, 1)
    g.vector.memset(T.M0[:, :], 0.0).then_inc(S.vm, 1)
    g.vector.memset(T.Q[0:96, 136:256], 0.0).then_inc(S.vr, 1)
    g.vector.memset(T.XE[:, 0:4], 0.0).then_inc(S.vx, 1)
    g.vector.memset(T.XE[:, 260:264], 0.0).then_inc(S.vx, 1)
    nw = _fills(g, T, W_FILLS[:1], S.vc, 0)

    g.sync.dma_start(T.XE[:, 4:260], x[:, :]).then_inc(S.ldx, 16)
    g.sync.wait_ge(S.vp1, 3)
    g.sync.dma_start(T.D1[0:64 * 67], T.Q[0:64, 69:136]).then_inc(S.std1, 16)
    g.sync.wait_ge(S.vq, 2)
    g.sync.dma_start(T.Q[120:122, :], x[0:2, :]).then_inc(S.ldq, 16)
    g.sync.dma_start(T.Q[127:128, 0:255], x[127:128, 1:256]).then_inc(S.ldq, 16)
    g.sync.dma_start(T.Q[123:124, 0:255], x[0:1, 1:256]).then_inc(S.ldq, 16)
    g.sync.wait_ge(S.vm, 2)
    g.sync.wait_ge(S.std1, 16)
    g.sync.dma_start(T.M1[0:64, 0:66], T.D1[0:64 * 66]).then_inc(S.ldm1, 16)
    g.sync.wait_ge(S.std0, 16)
    g.sync.dma_start(T.M0[0:64, 0:68], T.D0[0:64 * 68]).then_inc(S.ldm0, 16)

    g.scalar.wait_ge(S.vq, 2)
    g.scalar.dma_start(T.Q[96:120, :], x[96:120, :]).then_inc(S.ldq, 16)
    g.scalar.dma_start(T.Q[124:126, :], x[126:128, :]).then_inc(S.ldq, 16)
    g.scalar.dma_start(T.Q[126:127, 1:256], x[127:128, 0:255]).then_inc(S.ldq, 16)
    g.scalar.dma_start(T.Q[122:123, 1:256], x[0:1, 0:255]).then_inc(S.ldq, 16)
    g.scalar.wait_ge(S.vp0, 4)
    g.scalar.dma_start(T.D0[0:64 * 69], T.Q[0:64, 0:69]).then_inc(S.std0, 16)
    g.scalar.wait_ge(S.vm, 2)
    g.scalar.wait_ge(S.std1, 16)
    g.scalar.dma_start(T.M1[64:128, 64:130], T.D1[0:64 * 66]).then_inc(S.ldm1, 16)
    g.scalar.wait_ge(S.std0, 16)
    g.scalar.dma_start(T.M0[64:128, 64:132], T.D0[0:64 * 68]).then_inc(S.ldm0, 16)

    g.vector.wait_ge(S.vx, 2)
    g.vector.wait_ge(S.ldx, 16)
    g.vector.tensor_tensor(out=T.Z1[:, :], in0=T.XE[:, 3:259], in1=T.XE[:, 5:261], op=add).then_inc(S.vz1, 1)
    nw = _fills(g, T, W_FILLS[1:], S.vc, nw)
    g.vector.tensor_tensor(out=T.Z2[:, :], in0=T.XE[:, 2:258], in1=T.XE[:, 6:262], op=add).then_inc(S.vz2, 1)

    g.wait_ge(S.ldx, 16)
    g.remote_dma_fused([
        RemoteDMATransfer(dst_ids=[did(nb(0, -1)), did(nb(1, -1))], dma_engine_mask=0x0F, remote_sem=S.arrh,
                          srcs=[T.XE[:, 4:6]], dsts=[T.HB[:, 2:4], T.DB[:, 2:4]], alu_op=0),
        RemoteDMATransfer(dst_ids=[did(nb(0, 1)), did(nb(1, 1))], dma_engine_mask=0xF0, remote_sem=S.arrh,
                          srcs=[T.XE[:, 258:260]], dsts=[T.HB[:, 0:2], T.DB[:, 0:2]], alu_op=0),
    ], local_sem=S.sent)
    g.wait_ge(S.vp0, 4)
    g.wait_ge(S.vp1, 3)
    g.wait_ge(S.vr, 1)
    g.wait_ge(S.vq, 2)
    g.wait_ge(S.ldq, 112)
    rid, pid, _ = topo.addr(nb(1, 0))
    g.remote_dma(T.QL[:, :], T.Q[:, :], S.arrq, S.sent, pid, rid, 0xFFFF)

    pe = g.tensor
    pe.wait_ge(S.ldm1, 32)
    pe.wait_ge(S.vz1, 1)
    pe.matmul(out=T.P[:, :], lhsT=T.M1[:, 1:129], rhs=T.Z1[:, :], start=True, stop=False)
    pe.wait_ge(S.ldx, 16)
    pe.wait_ge(S.ldm0, 32)
    pe.matmul(out=T.P[:, :], lhsT=T.M0[:, 2:130], rhs=T.XE[:, 4:260], start=False, stop=False)
    pe.wait_ge(S.vc, nw)
    pe.wait_ge(S.arrq, 16)
    pe.matmul(out=T.P[:, :], lhsT=T.LQ[96:128, :], rhs=T.QL[96:128, :], start=False, stop=False)
    pe.wait_ge(S.arrh, 16)
    pe.matmul(out=T.P[:, 0:256:255], lhsT=T.M1[:, 1:129], rhs=T.HB[:, 1:3], start=False, stop=False)
    pe.matmul(out=T.P[:, 0:256:255], lhsT=T.CC[:, :], rhs=T.DB[:, 1:3], start=False, stop=True).then_inc(S.pe, 1)

    g.vector.wait_ge(S.vz2, 1)
    g.vector.wait_ge(S.arrh, 16)
    g.vector.tensor_tensor(out=T.Z2[:, 0:2], in0=T.Z2[:, 0:2], in1=T.HB[:, 0:2], op=add).then_inc(S.ve, 1)
    g.vector.tensor_tensor(out=T.Z2[:, 254:256], in0=T.Z2[:, 254:256], in1=T.HB[:, 2:4], op=add).then_inc(S.ve, 1)
    g.vector.wait_ge(S.ve, 2)
    g.vector.wait_ge(S.pe, 1)
    g.vector.tensor_tensor(out=T.Y[:, :], in0=T.P[:, :], in1=T.Z2[:, :], op=add).then_inc(S.vy, 1)

    g.sync.wait_ge(S.vy, 1)
    g.sync.dma_start(T.y[:, :], T.Y[:, :]).then_inc(S.st, 16)
    g.sync.wait_ge(S.st, 16)
    g.wait_ge(S.sent, 24)
